import numpy as np
import ml_dtypes

BF16 = ml_dtypes.bfloat16


def bf(x):
    return np.asarray(x, np.float32).astype(BF16)


def f32(x):
    return np.asarray(x, np.float32)


def f64(x):
    return np.asarray(x).astype(np.float64)


def striped(idx):
    return np.concatenate([l.reshape(-1, 16).T for l in idx])


def rows(idx, k):
    return np.tile(np.repeat(idx, 16, axis=0), (k // (16 * 8), 1))


def look(tab, idx):
    return np.take_along_axis(f64(tab), rows(idx, len(tab)), axis=1)


K, S, D, V, N = 256, 2048, 2, 512, 1024


def setup_inputs():
    return {"tab": f32(np.random.standard_normal((K, S))), "u0": f32(np.random.uniform(0.2, 1.0, (K, V))), "u1": f32(np.random.uniform(0.2, 1.0, (K, V))), "offs": striped(np.stack([np.random.permutation(S)[:N] for _ in range(8)]))}


def reference(tab, u0, u1, offs):
    idx = np.stack([g.T.reshape(-1) for g in np.split(offs, 8)])
    x = f64(u0) * np.minimum(np.maximum(look(tab, idx[:, :V]), -1.25), 1.0) + f64(u1) * np.minimum(np.maximum(look(tab, idx[:, 1 * V:2 * V]), -1.25), 1.0)
    return x

@@ -1,0 +1,48 @@
+import concourse.mybir as mybir
+
+F32 = mybir.dt.float32
+U16 = mybir.dt.uint16
+ADD, MULT = mybir.AluOpType.add, mybir.AluOpType.mult
+MAX, MIN = mybir.AluOpType.max, mybir.AluOpType.min
+
+P = 128
+LOW, HIGH = -1.25, 1.0
+PER_COLUMN = 16
+
+
+def tile_lookup_clipmix_out_kernel(tc, tab, u0, u1, offs, out):
+    nc = tc.nc
+    rows, table_cols = tab.shape
+    cols = u0.shape[1]
+    blocks = range(rows // P)
+    weights = (u0, u1)
+    pieces = range(len(weights))
+    piece_cols = cols // PER_COLUMN
+
+    with tc.tile_pool(name="held", bufs=1) as held:
+        lists = held.tile([P, offs.shape[1]], U16, name="lists")
+        nc.sync.dma_start(lists[:], offs)
+
+        table = [held.tile([P, table_cols], F32, name=f"table{b}") for b in blocks]
+        for b in blocks:
+            nc.sync.dma_start(table[b][:], tab[b * P:(b + 1) * P, :])
+        weight = {}
+        for b in blocks:
+            for d in pieces:
+                weight[b, d] = held.tile([P, cols], F32, name=f"weight{b}{d}")
+                nc.sync.dma_start(weight[b, d][:], weights[d][b * P:(b + 1) * P, :])
+
+        clamped = {}
+        for b in blocks:
+            for d in pieces:
+                clamped[b, d] = held.tile([P, cols], F32, name=f"clamped{b}{d}")
+                offsets = lists[:, d * piece_cols:(d + 1) * piece_cols]
+                nc.vector.tensor_scalar(clamped[b, d][:], table[b][:].indirect(offsets), LOW, HIGH, MAX, MIN)
+
+        for b in blocks:
+            product = [held.tile([P, cols], F32, name=f"product{b}{d}") for d in pieces]
+            for d in pieces:
+                nc.vector.tensor_tensor(product[d][:], clamped[b, d][:], weight[b, d][:], MULT)
+            total = held.tile([P, cols], F32, name=f"total{b}")
+            nc.vector.tensor_tensor(total[:], product[0][:], product[1][:], ADD)
+            nc.sync.dma_start(out[b * P:(b + 1) * P, :], total[:])

@@ -23,26 +23,24 @@ def tile_lookup_clipmix_out_kernel(tc, tab, u0, u1, offs, out):
         lists = held.tile([P, offs.shape[1]], U16, name="lists")
         nc.sync.dma_start(lists[:], offs)
 
-        table = [held.tile([P, table_cols], F32, name=f"table{b}") for b in blocks]
+        table, weight = {}, {}
         for b in blocks:
+            table[b] = held.tile([P, table_cols], F32, name=f"table{b}")
             nc.sync.dma_start(table[b][:], tab[b * P:(b + 1) * P, :])
-        weight = {}
-        for b in blocks:
             for d in pieces:
                 weight[b, d] = held.tile([P, cols], F32, name=f"weight{b}{d}")
                 nc.sync.dma_start(weight[b, d][:], weights[d][b * P:(b + 1) * P, :])
 
-        clamped = {}
         for b in blocks:
+            clamped = [held.tile([P, cols], F32, name=f"clamped{b}{d}") for d in pieces]
             for d in pieces:
-                clamped[b, d] = held.tile([P, cols], F32, name=f"clamped{b}{d}")
                 offsets = lists[:, d * piece_cols:(d + 1) * piece_cols]
-                nc.vector.tensor_scalar(clamped[b, d][:], table[b][:].indirect(offsets), LOW, HIGH, MAX, MIN)
+                nc.vector.tensor_scalar(clamped[d][:], table[b][:].indirect(offsets), LOW, HIGH, MAX, MIN)
 
-        for b in blocks:
             product = [held.tile([P, cols], F32, name=f"product{b}{d}") for d in pieces]
-            for d in pieces:
-                nc.vector.tensor_tensor(product[d][:], clamped[b, d][:], weight[b, d][:], MULT)
+            nc.gpsimd.tensor_tensor(product[0][:], clamped[0][:], weight[b, 0][:], MULT)
+            nc.vector.tensor_tensor(product[1][:], clamped[1][:], weight[b, 1][:], MULT)
             total = held.tile([P, cols], F32, name=f"total{b}")
-            nc.vector.tensor_tensor(total[:], product[0][:], product[1][:], ADD)
+            sum_engine = nc.vector if b == blocks[-1] else nc.gpsimd
+            sum_engine.tensor_tensor(total[:], product[0][:], product[1][:], ADD)
             nc.sync.dma_start(out[b * P:(b + 1) * P, :], total[:])

import concourse.mybir as mybir

F32 = mybir.dt.float32
U16 = mybir.dt.uint16
ADD, MULT = mybir.AluOpType.add, mybir.AluOpType.mult
MAX, MIN = mybir.AluOpType.max, mybir.AluOpType.min

P = 128
LOW, HIGH = -1.25, 1.0
PER_COLUMN = 16


def tile_lookup_clipmix_out_kernel(tc, tab, u0, u1, offs, out):
    nc = tc.nc
    rows, table_cols = tab.shape
    cols = u0.shape[1]
    blocks = range(rows // P)
    weights = (u0, u1)
    pieces = range(len(weights))
    piece_cols = cols // PER_COLUMN

    with tc.tile_pool(name="held", bufs=1) as held:
        lists = held.tile([P, offs.shape[1]], U16, name="lists")
        nc.sync.dma_start(lists[:], offs)

        table, weight = {}, {}
        for b in blocks:
            table[b] = held.tile([P, table_cols], F32, name=f"table{b}")
            nc.sync.dma_start(table[b][:], tab[b * P:(b + 1) * P, :])
            for d in pieces:
                weight[b, d] = held.tile([P, cols], F32, name=f"weight{b}{d}")
                nc.sync.dma_start(weight[b, d][:], weights[d][b * P:(b + 1) * P, :])

        for b in blocks:
            clamped = [held.tile([P, cols], F32, name=f"clamped{b}{d}") for d in pieces]
            for d in pieces:
                offsets = lists[:, d * piece_cols:(d + 1) * piece_cols]
                nc.vector.tensor_scalar(clamped[d][:], table[b][:].indirect(offsets), LOW, HIGH, MAX, MIN)

            product = [held.tile([P, cols], F32, name=f"product{b}{d}") for d in pieces]
            nc.gpsimd.tensor_tensor(product[0][:], clamped[0][:], weight[b, 0][:], MULT)
            nc.vector.tensor_tensor(product[1][:], clamped[1][:], weight[b, 1][:], MULT)
            total = held.tile([P, cols], F32, name=f"total{b}")
            sum_engine = nc.vector if b == blocks[-1] else nc.gpsimd
            sum_engine.tensor_tensor(total[:], product[0][:], product[1][:], ADD)
            nc.sync.dma_start(out[b * P:(b + 1) * P, :], total[:])
